import numpy as np
import ml_dtypes


def mxq(x, axis, fmt="e4m3"):
    dtype, down = {"e4m3": (ml_dtypes.float8_e4m3fn, 7), "e5m2": (ml_dtypes.float8_e5m2, 14)}[fmt]
    v = np.moveaxis(np.asarray(x, np.float32).astype(ml_dtypes.bfloat16).astype(np.float64), axis, -1)
    blocks = v.reshape(v.shape[:-1] + (-1, 32))
    amax = np.abs(blocks).max(-1, keepdims=True)
    byte = np.maximum(np.where(amax > 0, np.frexp(amax)[1] - 1 + 127, 0) - down, 1)
    scale = np.exp2(byte - 127.0)
    codes = (blocks / scale).astype(np.float32).astype(dtype).astype(np.float64)
    return np.moveaxis((codes * scale).reshape(v.shape), -1, axis)


WIDE = False


def mx_kscale(k):
    if not WIDE:
        return np.ones(k)
    levels = np.array([10, -10, 5, -5, 0])
    if k % 512:
        return np.exp2(np.random.permutation(np.resize(levels, k // 32))).repeat(32)
    a = np.empty((k // 512, 16))
    for p in range(k // 512):
        a[p, :8] = np.random.permutation(np.resize(levels, 8))
        for g in range(8):
            far = levels[np.abs(levels - a[p, g]) >= 10]
            a[p, g + 8] = far[np.random.randint(len(far))]
    return np.exp2(a.ravel()).repeat(32)


def f64(x):
    return np.asarray(x).astype(np.float64)


def striped(idx):
    return np.tile(idx.reshape(-1, 16).T, (8, 1)).astype(np.uint16)


def unstriped(offs):
    return offs[:16].T.reshape(-1).astype(np.int64)


E2M1 = np.array([0.0, 0.5, 1.0, 1.5, 2.0, 3.0, 4.0, 6.0, -0.0, -0.5, -1.0, -1.5, -2.0, -3.0, -4.0, -6.0])


def pack_weight(w, fmt):
    k, n = w.shape
    w = f64(np.asarray(w, np.float32).astype(ml_dtypes.bfloat16)).reshape(k // 32, 32, n)
    amax = np.abs(w).max(1)
    if fmt == "e4m3":
        byte = np.frexp(amax)[1] - 1 + 127 - 7
    else:
        mant, ex = np.frexp(amax / 6.0)
        byte = np.where(mant > 0.5, ex, ex - 1) + 127
    byte = np.clip(np.where(amax > 0, byte, 1), 1, 254)
    scaled = (w * np.exp2(127.0 - byte)[:, None, :]).reshape(k, n).astype(np.float32)
    by_word = np.ascontiguousarray(scaled.reshape(k // 512, 128, 4, n).transpose(0, 1, 3, 2))
    if fmt == "e4m3":
        words = by_word.astype(ml_dtypes.float8_e4m3fn).view(np.uint8)
    else:
        c = by_word.astype(ml_dtypes.float4_e2m1fn).view(np.uint8) & 0xF
        words = (c[..., 0::2] | (c[..., 1::2] << 4)).reshape(k // 512, 128, 2 * n)
    return np.ascontiguousarray(words), np.ascontiguousarray(byte.astype(np.uint8).reshape(k // 512, 16, n))


def unpack_weight(words, scales, fmt):
    g, _, n = scales.shape
    words = np.ascontiguousarray(words).reshape(g, 128, n, -1)
    if fmt == "e4m3":
        vals = words.view(ml_dtypes.float8_e4m3fn).astype(np.float64)
    else:
        nib = np.empty((g, 128, n, 4), np.uint8)
        nib[..., 0::2] = words & 0xF
        nib[..., 1::2] = words >> 4
        vals = E2M1[nib]
    vals = vals * np.repeat(np.exp2(scales.astype(np.float64) - 127.0), 8, axis=1)[..., None]
    return vals.transpose(0, 1, 3, 2).reshape(g * 512, n)


def gelu(v):
    return 0.5 * v * (1.0 + np.tanh(np.sqrt(2.0 / np.pi) * (v + 0.044715 * v**3)))


K, H, T, S, S1, S2, S3 = 1024, 512, 4096, 2048, 1024, 512, 256

def setup_inputs():
    n = np.random.standard_normal
    s = mx_kscale(K)[:, None]
    u = mx_kscale(H)[:, None]
    stance = np.sign(n((K, 1)))
    lean = np.random.uniform(-1.0, 1.0, (1, T))
    turn = np.random.uniform(0.5, 2.2, (1, H))
    tab_words, tab_scales = pack_weight((stance * lean + n((K, T))) * s, "e4m3")
    w1 = (0.12 * n((K, H)) / np.sqrt(K) + stance * turn / K) / s
    w4_words, w4_scales = pack_weight(2.0 * n((H, H)) / np.sqrt(H) / u, "e2m1")
    return {
        "tab_words": tab_words, "tab_scales": tab_scales,
        "w1": w1.astype(np.float32),
        "w4_words": w4_words, "w4_scales": w4_scales,
        "gain": (np.exp(0.3 * n(H)) * u[:, 0]).astype(np.float32),
        "offs": striped(np.random.permutation(T)[:S]),
        "pos1": striped(np.random.permutation(S)[:S1]),
        "pos2": striped(np.random.permutation(S)[:S1]),
        "pos3": striped(np.random.permutation(S1)[:S2]),
        "pos4": striped(np.random.permutation(S1)[:S2]),
        "pos5": striped(np.random.permutation(S2)[:S3]),
        "pos6": striped(np.random.permutation(S2)[:S3]),
    }

def reference(tab_words, tab_scales, w1, w4_words, w4_scales, gain, offs, pos1, pos2, pos3, pos4, pos5, pos6):
    v = unpack_weight(tab_words, tab_scales, "e4m3")[:, unstriped(offs)]
    w4 = unpack_weight(w4_words, w4_scales, "e2m1")
    h = np.cos(mxq(f64(w1), 0, "e4m3").T @ v)
    a1 = h[:, unstriped(pos1)] * h[:, unstriped(pos2)]
    a2 = np.maximum(a1[:, unstriped(pos3)], a1[:, unstriped(pos4)])
    a3 = a2[:, unstriped(pos5)] + a2[:, unstriped(pos6)]
    z = f64(gain)[:, None] * np.tanh(a3)
    y = w4.T @ mxq(z, 0, "e4m3")
    return y + a3

@@ -1,0 +1,254 @@
+import math
+from contextlib import ExitStack
+
+import concourse.mybir as mybir
+from concourse.masks import make_identity
+
+K, H, T, S, S1, S2, S3 = 1024, 512, 4096, 2048, 1024, 512, 256
+FLOPS = 2 * K * H * S + 2 * H * H * S3
+
+F32 = mybir.dt.float32
+BF16 = mybir.dt.bfloat16
+I32 = mybir.dt.int32
+U32 = mybir.dt.uint32
+U16 = mybir.dt.uint16
+U8 = mybir.dt.uint8
+FP8X4 = mybir.dt.float8_e4m3fn_x4
+FP4X4 = mybir.dt.float4_e2m1fn_x4
+ALU = mybir.AluOpType
+ACT = mybir.ActivationFunctionType
+
+P = 128
+PACK = 4
+PASSES = K // (P * PACK)
+BANK = 512
+SLICES = S // BANK
+BLOCKS = BANK // P
+QUADRANTS = 4
+TURN = 1.0 / (2.0 * math.pi)
+
+
+def tile_list_committee_award_scores_kernel(
+    tc, tab_words, tab_scales, w1, w4_words, w4_scales, gain, offs, pos1, pos2, pos3, pos4, pos5, pos6, out
+):
+    nc = tc.nc
+    with ExitStack() as ctx:
+        lists = ctx.enter_context(tc.tile_pool(name="lists", bufs=1))
+        keep = ctx.enter_context(tc.tile_pool(name="keep", bufs=1))
+        ring = ctx.enter_context(tc.tile_pool(name="ring", bufs=3))
+        psum = ctx.enter_context(tc.psum_pool(name="psum", bufs=1))
+
+        def load_list(src, name):
+            tile = lists.tile(list(src.shape), U16, name=name)
+            nc.sync.dma_start(tile[:], src)
+            return tile
+
+        scale_window = keep.tile([P, T], U8, name="scale_window", align_bytes=64)
+        nc.vector.memset(scale_window[:].bitcast(I32), 0)
+        for q in range(QUADRANTS):
+            nc.gpsimd.dma_start(
+                scale_window[32 * q : 32 * q + 4 * PASSES, :].bitcast(I32),
+                tab_scales[:, 4 * q : 4 * q + 4, :].bitcast(I32),
+            )
+        offs_t = load_list(offs, "offs_t")
+        word_window = []
+        for a in range(PASSES):
+            win = keep.tile([P, T], I32, name=f"word_window{a}", align_bytes=64)
+            nc.sync.dma_start(win[:], tab_words[a].rearrange("p t i -> p (t i)").bitcast(I32))
+            word_window.append(win)
+        w1_raw = []
+        for a in range(PASSES):
+            raw = keep.tile([P, PACK, H], F32, name=f"w1_raw{a}", align_bytes=64)
+            nc.sync.dma_start(raw[:], w1[512 * a : 512 * (a + 1), :].rearrange("(p i) c -> p i c", i=PACK))
+            w1_raw.append(raw)
+        p1, p2 = load_list(pos1, "p1"), load_list(pos2, "p2")
+        w4_raw = keep.tile([P, 2 * H], U8, name="w4_raw", align_bytes=64)
+        nc.sync.dma_start(w4_raw[:].bitcast(I32), w4_words[0].bitcast(I32))
+        w4_scale_raw = keep.tile([P, H], U8, name="w4_scale_raw", align_bytes=64)
+        nc.vector.memset(w4_scale_raw[:].bitcast(I32), 0)
+        for q in range(QUADRANTS):
+            nc.sync.dma_start(
+                w4_scale_raw[32 * q : 32 * q + 4, :].bitcast(I32), w4_scales[0, 4 * q : 4 * q + 4, :].bitcast(I32)
+            )
+        p3, p4 = load_list(pos3, "p3"), load_list(pos4, "p4")
+        p5, p6 = load_list(pos5, "p5"), load_list(pos6, "p6")
+        gain_t = keep.tile([P, PACK], F32, name="gain_t")
+        nc.sync.dma_start(gain_t[:], gain.rearrange("(p t) -> p t", t=PACK))
+        ident = keep.tile([P, P], F32, name="ident")
+        make_identity(nc, ident[:])
+
+        v_scales = keep.tile([P, S], U8, name="v_scales", align_bytes=64)
+        v_words = [keep.tile([P, S], U32, name=f"v_words{a}", align_bytes=64) for a in range(PASSES)]
+        nc.vector.tensor_copy(v_words[0][:], word_window[0][:].bitcast(U32).indirect(offs_t[:]))
+        cols_per_slice = BANK // 16
+        for s in range(SLICES):
+            nc.vector.tensor_copy(
+                v_scales[:, s * BANK : (s + 1) * BANK],
+                scale_window[:].indirect(offs_t[:, s * cols_per_slice : (s + 1) * cols_per_slice]),
+            )
+        for s in range(SLICES):
+            nc.vector.tensor_copy(
+                v_words[1][:, s * BANK : (s + 1) * BANK],
+                word_window[1][:].bitcast(U32).indirect(offs_t[:, s * cols_per_slice : (s + 1) * cols_per_slice]),
+            )
+
+        w1_codes, w1_scales = {}, {}
+
+        def quantize_w1(t):
+            for a in range(PASSES):
+                grouped = keep.tile([P, P, PACK], BF16, name=f"grouped{a}{t}", align_bytes=64)
+                nc.scalar.copy(grouped[:], w1_raw[a][:].rearrange("p i (m t) -> p t m i", t=PACK)[:, t])
+                codes = keep.tile([P, P], U32, name=f"w1_codes{a}{t}", align_bytes=64)
+                scales = keep.tile([P, P], U8, name=f"w1_scales{a}{t}", align_bytes=64)
+                nc.vector.quantize_mx(
+                    out=codes[:].bitcast(FP8X4), scales=scales[:], in_=grouped[:].rearrange("p m i -> p (m i)")
+                )
+                w1_codes[a, t], w1_scales[a, t] = codes, scales
+
+        h = [keep.tile([P, S], F32, name=f"h{t}", tag=f"h{t}", align_bytes=64) for t in range(PACK)]
+
+        quantize_w1(0)
+        direct = [psum.tile([P, BANK], F32, name=f"direct{s}", tag=f"bank{s}") for s in range(SLICES)]
+        for a in range(PASSES):
+            for s in range(SLICES):
+                cols = slice(s * BANK, (s + 1) * BANK)
+                nc.tensor.matmul_mx(
+                    out=direct[s][:],
+                    lhsT=w1_codes[a, 0][:].bitcast(FP8X4),
+                    lhsT_scale=w1_scales[a, 0][:],
+                    rhs=v_words[a][:, cols].bitcast(FP8X4),
+                    rhs_scale=v_scales[4 * a :, cols],
+                    start=(a == 0),
+                    stop=(a == PASSES - 1),
+                )
+        for s in range(SLICES):
+            cols = slice(s * BANK, (s + 1) * BANK)
+            turns = ring.tile([P, BANK], F32, name="turns", tag="turns")
+            whole = ring.tile([P, BANK], U32, name="whole", tag="whole")
+            rest = ring.tile([P, BANK], F32, name="rest", tag="rest")
+            nc.scalar.activation(turns[:], direct[s][:], ACT.Abs, scale=TURN)
+            nc.scalar.activation(whole[:], turns[:], ACT.Copy, bias=-0.25)
+            nc.vector.scalar_tensor_tensor(
+                rest[:], turns[:], 0.25, whole[:].bitcast(I32), ALU.subtract, ALU.subtract
+            )
+            nc.scalar.activation(h[0][:, cols], rest[:], ACT.Sin, scale=-2.0 * math.pi)
+
+        for t in range(1, PACK):
+            quantize_w1(t)
+
+        w4_codes = keep.tile([P, 2 * H], U8, name="w4_codes", align_bytes=64)
+        nc.vector.tensor_copy(
+            w4_codes[:].rearrange("p (t m b) -> p t m b", t=PACK, b=2),
+            w4_raw[:].rearrange("p (m t b) -> p t m b", t=PACK, b=2),
+        )
+        w4_scale = keep.tile([P, H], U8, name="w4_scale", align_bytes=64)
+        nc.vector.tensor_copy(
+            w4_scale[:].rearrange("p (t m) -> p t m", t=PACK), w4_scale_raw[:].rearrange("p (m t) -> p t m", t=PACK)
+        )
+
+        a3 = keep.tile([P, PACK, S3], F32, name="a3", align_bytes=64)
+
+        def levels(t):
+            left1 = ring.tile([P, S1], F32, name="left1", tag="left1", bufs=2)
+            a1 = ring.tile([P, S1], F32, name="a1", tag="a1", bufs=2)
+            nc.vector.tensor_copy(left1[:], h[t][:].indirect(p1[:]))
+            nc.vector.tensor_tensor(a1[:], h[t][:].indirect(p2[:]), left1[:], ALU.mult)
+            left2 = ring.tile([P, S2], F32, name="left2", tag="left2", bufs=2)
+            right2 = ring.tile([P, S2], F32, name="right2", tag="right2", bufs=2)
+            a2 = ring.tile([P, S2], F32, name="a2", tag="a2", bufs=2)
+            nc.vector.tensor_copy(left2[:], a1[:].indirect(p3[:]))
+            nc.vector.tensor_copy(right2[:], a1[:].indirect(p4[:]))
+            nc.vector.tensor_tensor(a2[:], left2[:], right2[:], ALU.max)
+            left3 = ring.tile([P, S3], F32, name="left3", tag="left3", bufs=2)
+            nc.vector.tensor_copy(left3[:], a2[:].indirect(p5[:]))
+            nc.vector.tensor_tensor(a3[:, t, :], a2[:].indirect(p6[:]), left3[:], ALU.add)
+
+        levels(0)
+
+        units = [(t, s) for t in range(1, PACK) for s in range(SLICES)]
+        state = {}
+
+        def multiply(u):
+            t, s = units[u]
+            bank = psum.tile([P, BLOCKS, P], F32, name="product", tag=f"bank{4 + u % 2}")
+            for b in range(BLOCKS):
+                cols = slice(s * BANK + b * P, s * BANK + (b + 1) * P)
+                for a in range(PASSES):
+                    nc.tensor.matmul_mx(
+                        out=bank[:, b, :],
+                        lhsT=v_words[a][:, cols].bitcast(FP8X4),
+                        lhsT_scale=v_scales[4 * a :, cols],
+                        rhs=w1_codes[a, t][:].bitcast(FP8X4),
+                        rhs_scale=w1_scales[a, t][:],
+                        start=(a == 0),
+                        stop=(a == PASSES - 1),
+                    )
+            turns = ring.tile([P, BANK], F32, name="turns", tag="turns")
+            nc.scalar.activation(turns[:], bank[:].rearrange("p b m -> p (b m)"), ACT.Abs, scale=TURN)
+            state[u] = turns
+
+        def count(u):
+            turns = state[u]
+            whole = ring.tile([P, BANK], U32, name="whole", tag="whole")
+            nc.scalar.activation(whole[:], turns[:], ACT.Copy, bias=-0.25)
+            state[u] = (turns, whole)
+
+        def subtract(u):
+            turns, whole = state[u]
+            minus = ring.tile([P, BANK], F32, name="minus", tag="rest")
+            nc.scalar.activation(minus[:], whole[:], ACT.Copy, scale=-1.0, bias=-0.25)
+            bank = psum.tile([P, BLOCKS, P], F32, name="turned", tag=f"bank{6 + u % 2}")
+            for b in range(BLOCKS):
+                cols = slice(b * P, (b + 1) * P)
+                nc.tensor.matmul(bank[:, b, :], turns[:, cols], ident[:], start=True, stop=False, is_transpose=True)
+                nc.tensor.matmul(bank[:, b, :], minus[:, cols], ident[:], start=False, stop=True, is_transpose=True)
+            state[u] = bank
+
+        def cosine(u):
+            t, s = units[u]
+            nc.scalar.activation(
+                h[t][:, s * BANK : (s + 1) * BANK],
+                state[u][:].rearrange("p b m -> p (b m)"),
+                ACT.Sin,
+                scale=-2.0 * math.pi,
+            )
+            if s == SLICES - 1:
+                levels(t)
+
+        stages = [multiply, count, subtract, cosine]
+        for step in range(len(units) + len(stages) - 1):
+            for lag in reversed(range(len(stages))):
+                u = step - lag
+                if 0 <= u < len(units):
+                    stages[lag](u)
+
+        z32 = keep.tile([P, PACK, S3], F32, name="z32", align_bytes=64)
+        squashed = keep.tile([P, PACK, S3], F32, name="squashed", tag=f"h{PACK - 1}", align_bytes=64)
+        for t in range(PACK):
+            nc.scalar.activation(squashed[:, t, :], a3[:, t, :], ACT.Tanh)
+            nc.scalar.activation(z32[:, t, :], squashed[:, t, :], ACT.Copy, scale=gain_t[:, t : t + 1])
+        z16 = keep.tile([P, S3, PACK], BF16, name="z16", align_bytes=64)
+        nc.vector.tensor_copy(z16[:], z32[:].rearrange("p t j -> p j t"))
+        z_codes = keep.tile([P, S3], U32, name="z_codes", align_bytes=64)
+        z_scales = keep.tile([P, S3], U8, name="z_scales", align_bytes=64)
+        nc.vector.quantize_mx(
+            out=z_codes[:].bitcast(FP8X4), scales=z_scales[:], in_=z16[:].rearrange("p j t -> p (j t)")
+        )
+        out_rows = out.rearrange("(p t) j -> p t j", t=PACK)
+        for half in range(2):
+            bank = psum.tile([P, 2, S3], F32, name="y", tag=f"bank{half}")
+            for i in range(2):
+                t = 2 * half + i
+                nc.tensor.matmul_mx(
+                    out=bank[:, i, :],
+                    lhsT=w4_codes[:, 2 * P * t : 2 * P * (t + 1)].bitcast(FP4X4),
+                    lhsT_scale=w4_scale[:, P * t : P * (t + 1)],
+                    rhs=z_codes[:].bitcast(FP8X4),
+                    rhs_scale=z_scales[:],
+                    start=True,
+                    stop=True,
+                )
+            result = keep.tile([P, 2, S3], F32, name=f"result{half}", align_bytes=64)
+            nc.vector.tensor_tensor(result[:], bank[:], a3[:, 2 * half : 2 * half + 2, :], ALU.add)
+            queue = nc.sync if half == 0 else nc.scalar
+            queue.dma_start(out_rows[:, 2 * half : 2 * half + 2, :], result[:])

@@ -25,6 +25,7 @@ BANK = 512
 SLICES = S // BANK
 BLOCKS = BANK // P
 QUADRANTS = 4
+SCALAR_SLICES = 3
 TURN = 1.0 / (2.0 * math.pi)
 
 
@@ -46,24 +47,27 @@ def tile_list_committee_award_scores_kernel(
         scale_window = keep.tile([P, T], U8, name="scale_window", align_bytes=64)
         nc.vector.memset(scale_window[:].bitcast(I32), 0)
         for q in range(QUADRANTS):
-            nc.gpsimd.dma_start(
+            nc.sync.dma_start(
                 scale_window[32 * q : 32 * q + 4 * PASSES, :].bitcast(I32),
                 tab_scales[:, 4 * q : 4 * q + 4, :].bitcast(I32),
             )
         offs_t = load_list(offs, "offs_t")
-        word_window = []
-        for a in range(PASSES):
+        w4_raw = keep.tile([P, 2 * H], U8, name="w4_raw", align_bytes=64)
+        nc.sync.dma_start(w4_raw[:].bitcast(I32), w4_words[0].bitcast(I32))
+
+        def load_words(a):
             win = keep.tile([P, T], I32, name=f"word_window{a}", align_bytes=64)
             nc.sync.dma_start(win[:], tab_words[a].rearrange("p t i -> p (t i)").bitcast(I32))
-            word_window.append(win)
+            return win
+
+        word_window = [load_words(0)]
         w1_raw = []
         for a in range(PASSES):
             raw = keep.tile([P, PACK, H], F32, name=f"w1_raw{a}", align_bytes=64)
             nc.sync.dma_start(raw[:], w1[512 * a : 512 * (a + 1), :].rearrange("(p i) c -> p i c", i=PACK))
             w1_raw.append(raw)
+        word_window.append(load_words(1))
         p1, p2 = load_list(pos1, "p1"), load_list(pos2, "p2")
-        w4_raw = keep.tile([P, 2 * H], U8, name="w4_raw", align_bytes=64)
-        nc.sync.dma_start(w4_raw[:].bitcast(I32), w4_words[0].bitcast(I32))
         w4_scale_raw = keep.tile([P, H], U8, name="w4_scale_raw", align_bytes=64)
         nc.vector.memset(w4_scale_raw[:].bitcast(I32), 0)
         for q in range(QUADRANTS):
@@ -76,16 +80,14 @@ def tile_list_committee_award_scores_kernel(
         nc.sync.dma_start(gain_t[:], gain.rearrange("(p t) -> p t", t=PACK))
         ident = keep.tile([P, P], F32, name="ident")
         make_identity(nc, ident[:])
+        warm = keep.tile([P, 1], F32, name="warm")
+        nc.scalar.activation(warm[:], ident[:, 0:1], ACT.Silu)
 
         v_scales = keep.tile([P, S], U8, name="v_scales", align_bytes=64)
         v_words = [keep.tile([P, S], U32, name=f"v_words{a}", align_bytes=64) for a in range(PASSES)]
         nc.vector.tensor_copy(v_words[0][:], word_window[0][:].bitcast(U32).indirect(offs_t[:]))
         cols_per_slice = BANK // 16
-        for s in range(SLICES):
-            nc.vector.tensor_copy(
-                v_scales[:, s * BANK : (s + 1) * BANK],
-                scale_window[:].indirect(offs_t[:, s * cols_per_slice : (s + 1) * cols_per_slice]),
-            )
+        nc.vector.tensor_copy(v_scales[:], scale_window[:].indirect(offs_t[:]))
         for s in range(SLICES):
             nc.vector.tensor_copy(
                 v_words[1][:, s * BANK : (s + 1) * BANK],
@@ -107,7 +109,8 @@ def tile_list_committee_award_scores_kernel(
 
         h = [keep.tile([P, S], F32, name=f"h{t}", tag=f"h{t}", align_bytes=64) for t in range(PACK)]
 
-        quantize_w1(0)
+        for t in range(PACK):
+            quantize_w1(t)
         direct = [psum.tile([P, BANK], F32, name=f"direct{s}", tag=f"bank{s}") for s in range(SLICES)]
         for a in range(PASSES):
             for s in range(SLICES):
@@ -123,45 +126,68 @@ def tile_list_committee_award_scores_kernel(
                 )
         for s in range(SLICES):
             cols = slice(s * BANK, (s + 1) * BANK)
-            turns = ring.tile([P, BANK], F32, name="turns", tag="turns")
             whole = ring.tile([P, BANK], U32, name="whole", tag="whole")
             rest = ring.tile([P, BANK], F32, name="rest", tag="rest")
-            nc.scalar.activation(turns[:], direct[s][:], ACT.Abs, scale=TURN)
-            nc.scalar.activation(whole[:], turns[:], ACT.Copy, bias=-0.25)
-            nc.vector.scalar_tensor_tensor(
-                rest[:], turns[:], 0.25, whole[:].bitcast(I32), ALU.subtract, ALU.subtract
-            )
-            nc.scalar.activation(h[0][:, cols], rest[:], ACT.Sin, scale=-2.0 * math.pi)
-
-        for t in range(1, PACK):
-            quantize_w1(t)
+            if s < SCALAR_SLICES:
+                turns = ring.tile([P, BANK], F32, name="turns", tag="turns")
+                nc.scalar.activation(turns[:], direct[s][:], ACT.Abs, scale=TURN)
+                nc.scalar.activation(whole[:], turns[:], ACT.Copy, bias=-0.25)
+                nc.vector.scalar_tensor_tensor(
+                    rest[:], turns[:], 0.25, whole[:].bitcast(I32), ALU.subtract, ALU.subtract
+                )
+                nc.scalar.activation(h[0][:, cols], rest[:], ACT.Sin, scale=-2.0 * math.pi)
+            else:
+                nc.vector.tensor_scalar(whole[:].bitcast(I32), direct[s][:], TURN, -0.25, ALU.mult, ALU.add)
+                nc.vector.scalar_tensor_tensor(
+                    rest[:], direct[s][:], TURN, whole[:].bitcast(I32), ALU.mult, ALU.subtract
+                )
+                nc.scalar.activation(h[0][:, cols], rest[:], ACT.Sin, scale=-2.0 * math.pi, bias=0.5 * math.pi)
 
         w4_codes = keep.tile([P, 2 * H], U8, name="w4_codes", align_bytes=64)
         nc.vector.tensor_copy(
             w4_codes[:].rearrange("p (t m b) -> p t m b", t=PACK, b=2),
             w4_raw[:].rearrange("p (m t b) -> p t m b", t=PACK, b=2),
         )
-        w4_scale = keep.tile([P, H], U8, name="w4_scale", align_bytes=64)
-        nc.vector.tensor_copy(
-            w4_scale[:].rearrange("p (t m) -> p t m", t=PACK), w4_scale_raw[:].rearrange("p (m t) -> p t m", t=PACK)
-        )
 
         a3 = keep.tile([P, PACK, S3], F32, name="a3", align_bytes=64)
 
+        a2 = {}
+        half1 = S1 // 2
+
+        def third_pick(t, cols):
+            left3 = ring.tile([P, cols.stop - cols.start], F32, name="left3", tag="left0", bufs=1)
+            nc.vector.tensor_copy(left3[:], a2[t][:].indirect(p5[:, cols.start // 16 : cols.stop // 16]))
+            return left3
+
+        def third_sum(t, cols, left3):
+            nc.vector.tensor_tensor(
+                a3[:, t, cols], a2[t][:].indirect(p6[:, cols.start // 16 : cols.stop // 16]), left3, ALU.add
+            )
+
         def levels(t):
-            left1 = ring.tile([P, S1], F32, name="left1", tag="left1", bufs=2)
             a1 = ring.tile([P, S1], F32, name="a1", tag="a1", bufs=2)
-            nc.vector.tensor_copy(left1[:], h[t][:].indirect(p1[:]))
-            nc.vector.tensor_tensor(a1[:], h[t][:].indirect(p2[:]), left1[:], ALU.mult)
+            left1 = []
+            for i in range(2):
+                left = ring.tile([P, half1], F32, name="left1", tag=f"left{i}", bufs=1)
+                nc.vector.tensor_copy(left[:], h[t][:].indirect(p1[:, i * half1 // 16 : (i + 1) * half1 // 16]))
+                left1.append(left)
+            for i in range(2):
+                nc.vector.tensor_tensor(
+                    a1[:, i * half1 : (i + 1) * half1],
+                    h[t][:].indirect(p2[:, i * half1 // 16 : (i + 1) * half1 // 16]),
+                    left1[i][:],
+                    ALU.mult,
+                )
+            if t > 0:
+                left3 = third_pick(t - 1, slice(0, S3))
             left2 = ring.tile([P, S2], F32, name="left2", tag="left2", bufs=2)
             right2 = ring.tile([P, S2], F32, name="right2", tag="right2", bufs=2)
-            a2 = ring.tile([P, S2], F32, name="a2", tag="a2", bufs=2)
+            a2[t] = ring.tile([P, S2], F32, name="a2", tag="a2", bufs=2)
             nc.vector.tensor_copy(left2[:], a1[:].indirect(p3[:]))
             nc.vector.tensor_copy(right2[:], a1[:].indirect(p4[:]))
-            nc.vector.tensor_tensor(a2[:], left2[:], right2[:], ALU.max)
-            left3 = ring.tile([P, S3], F32, name="left3", tag="left3", bufs=2)
-            nc.vector.tensor_copy(left3[:], a2[:].indirect(p5[:]))
-            nc.vector.tensor_tensor(a3[:, t, :], a2[:].indirect(p6[:]), left3[:], ALU.add)
+            if t > 0:
+                third_sum(t - 1, slice(0, S3), left3[:])
+            nc.vector.tensor_tensor(a2[t][:], left2[:], right2[:], ALU.max)
 
         levels(0)
 
@@ -222,33 +248,55 @@ def tile_list_committee_award_scores_kernel(
                 if 0 <= u < len(units):
                     stages[lag](u)
 
-        z32 = keep.tile([P, PACK, S3], F32, name="z32", align_bytes=64)
-        squashed = keep.tile([P, PACK, S3], F32, name="squashed", tag=f"h{PACK - 1}", align_bytes=64)
-        for t in range(PACK):
-            nc.scalar.activation(squashed[:, t, :], a3[:, t, :], ACT.Tanh)
-            nc.scalar.activation(z32[:, t, :], squashed[:, t, :], ACT.Copy, scale=gain_t[:, t : t + 1])
-        z16 = keep.tile([P, S3, PACK], BF16, name="z16", align_bytes=64)
-        nc.vector.tensor_copy(z16[:], z32[:].rearrange("p t j -> p j t"))
-        z_codes = keep.tile([P, S3], U32, name="z_codes", align_bytes=64)
-        z_scales = keep.tile([P, S3], U8, name="z_scales", align_bytes=64)
-        nc.vector.quantize_mx(
-            out=z_codes[:].bitcast(FP8X4), scales=z_scales[:], in_=z16[:].rearrange("p j t -> p (j t)")
+        last = PACK - 1
+        halves = [slice(i * P, (i + 1) * P) for i in range(S3 // P)]
+        left3 = keep.tile([P, S3], F32, name="left3_last", tag="late", align_bytes=64)
+        for cols in halves:
+            nc.vector.tensor_copy(left3[:, cols], a2[last][:].indirect(p5[:, cols.start // 16 : cols.stop // 16]))
+        for cols in halves:
+            third_sum(last, cols, left3[:, cols])
+        w4_scale = keep.tile([P, H], U8, name="w4_scale", tag="late", align_bytes=64)
+        nc.vector.tensor_copy(
+            w4_scale[:].rearrange("p (t m) -> p t m", t=PACK), w4_scale_raw[:].rearrange("p (m t) -> p t m", t=PACK)
         )
+        z32 = keep.tile([P, PACK, S3], F32, name="z32", align_bytes=64)
+        squashed = keep.tile([P, PACK, S3], F32, name="squashed", tag=f"h{last}", align_bytes=64)
+
+        def gained_tanh(t, cols):
+            nc.scalar.activation(squashed[:, t, cols], a3[:, t, cols], ACT.Tanh)
+            nc.scalar.activation(z32[:, t, cols], squashed[:, t, cols], ACT.Copy, scale=gain_t[:, t : t + 1])
+
+        for t in range(last):
+            gained_tanh(t, slice(0, S3))
+        for cols in halves:
+            gained_tanh(last, cols)
         out_rows = out.rearrange("(p t) j -> p t j", t=PACK)
-        for half in range(2):
-            bank = psum.tile([P, 2, S3], F32, name="y", tag=f"bank{half}")
-            for i in range(2):
-                t = 2 * half + i
-                nc.tensor.matmul_mx(
-                    out=bank[:, i, :],
-                    lhsT=w4_codes[:, 2 * P * t : 2 * P * (t + 1)].bitcast(FP4X4),
-                    lhsT_scale=w4_scale[:, P * t : P * (t + 1)],
-                    rhs=z_codes[:].bitcast(FP8X4),
-                    rhs_scale=z_scales[:],
-                    start=True,
-                    stop=True,
-                )
-            result = keep.tile([P, 2, S3], F32, name=f"result{half}", align_bytes=64)
-            nc.vector.tensor_tensor(result[:], bank[:], a3[:, 2 * half : 2 * half + 2, :], ALU.add)
-            queue = nc.sync if half == 0 else nc.scalar
-            queue.dma_start(out_rows[:, 2 * half : 2 * half + 2, :], result[:])
+        z16 = [keep.tile([P, P, PACK], BF16, name=f"z16_{i}", align_bytes=64) for i in range(len(halves))]
+        for i, cols in enumerate(halves):
+            nc.vector.tensor_copy(z16[i][:], z32[:, :, cols].rearrange("p t j -> p j t"))
+        banks = []
+        for i, cols in enumerate(halves):
+            z_codes = keep.tile([P, P], U32, name=f"z_codes{i}", align_bytes=64)
+            z_scales = keep.tile([P, P], U8, name=f"z_scales{i}", align_bytes=64)
+            nc.vector.quantize_mx(
+                out=z_codes[:].bitcast(FP8X4), scales=z_scales[:], in_=z16[i][:].rearrange("p j t -> p (j t)")
+            )
+            for pair in range(PACK // 2):
+                bank = psum.tile([P, 2, P], F32, name="y", tag=f"bank{2 * i + pair}")
+                for e in range(2):
+                    t = 2 * pair + e
+                    nc.tensor.matmul_mx(
+                        out=bank[:, e, :],
+                        lhsT=w4_codes[:, 2 * P * t : 2 * P * (t + 1)].bitcast(FP4X4),
+                        lhsT_scale=w4_scale[:, P * t : P * (t + 1)],
+                        rhs=z_codes[:].bitcast(FP8X4),
+                        rhs_scale=z_scales[:],
+                        start=True,
+                        stop=True,
+                    )
+                banks.append((bank, slice(2 * pair, 2 * pair + 2), cols))
+        for n, (bank, rows, cols) in enumerate(banks):
+            result = keep.tile([P, 2, P], F32, name=f"result{n}", align_bytes=64)
+            nc.vector.tensor_tensor(result[:], bank[:], a3[:, rows, cols], ALU.add)
+            queue = nc.sync if n % 2 == 0 else nc.scalar
+            queue.dma_start(out_rows[:, rows, cols], result[:])

@@ -36,7 +36,8 @@ def tile_list_committee_award_scores_kernel(
     with ExitStack() as ctx:
         lists = ctx.enter_context(tc.tile_pool(name="lists", bufs=1))
         keep = ctx.enter_context(tc.tile_pool(name="keep", bufs=1))
-        ring = ctx.enter_context(tc.tile_pool(name="ring", bufs=3))
+        ring = ctx.enter_context(tc.tile_pool(name="ring", bufs=4))
+        wide = ctx.enter_context(tc.tile_pool(name="wide", bufs=3))
         psum = ctx.enter_context(tc.psum_pool(name="psum", bufs=1))
 
         def load_list(src, name):
@@ -96,29 +97,29 @@ def tile_list_committee_award_scores_kernel(
 
         w1_codes, w1_scales = {}, {}
 
-        def quantize_w1(t):
-            for a in range(PASSES):
-                grouped = keep.tile([P, P, PACK], BF16, name=f"grouped{a}{t}", align_bytes=64)
-                nc.scalar.copy(grouped[:], w1_raw[a][:].rearrange("p i (m t) -> p t m i", t=PACK)[:, t])
-                codes = keep.tile([P, P], U32, name=f"w1_codes{a}{t}", align_bytes=64)
-                scales = keep.tile([P, P], U8, name=f"w1_scales{a}{t}", align_bytes=64)
-                nc.vector.quantize_mx(
-                    out=codes[:].bitcast(FP8X4), scales=scales[:], in_=grouped[:].rearrange("p m i -> p (m i)")
-                )
-                w1_codes[a, t], w1_scales[a, t] = codes, scales
+        for a in range(PASSES):
+            grouped = keep.tile([P, PACK, P, PACK], BF16, name=f"grouped{a}", align_bytes=64)
+            nc.scalar.copy(
+                grouped[:].rearrange("p t m i -> p m t i"), w1_raw[a][:].rearrange("p i (m t) -> p m t i", t=PACK)
+            )
+            codes = keep.tile([P, H], U32, name=f"w1_codes{a}", align_bytes=64)
+            scales = keep.tile([P, H], U8, name=f"w1_scales{a}", align_bytes=64)
+            nc.vector.quantize_mx(
+                out=codes[:].bitcast(FP8X4), scales=scales[:], in_=grouped[:].rearrange("p t m i -> p (t m i)")
+            )
+            for t in range(PACK):
+                w1_codes[a, t], w1_scales[a, t] = codes[:, t * P : (t + 1) * P], scales[:, t * P : (t + 1) * P]
 
         h = [keep.tile([P, S], F32, name=f"h{t}", tag=f"h{t}", align_bytes=64) for t in range(PACK)]
 
-        for t in range(PACK):
-            quantize_w1(t)
         direct = [psum.tile([P, BANK], F32, name=f"direct{s}", tag=f"bank{s}") for s in range(SLICES)]
         for a in range(PASSES):
             for s in range(SLICES):
                 cols = slice(s * BANK, (s + 1) * BANK)
                 nc.tensor.matmul_mx(
                     out=direct[s][:],
-                    lhsT=w1_codes[a, 0][:].bitcast(FP8X4),
-                    lhsT_scale=w1_scales[a, 0][:],
+                    lhsT=w1_codes[a, 0].bitcast(FP8X4),
+                    lhsT_scale=w1_scales[a, 0],
                     rhs=v_words[a][:, cols].bitcast(FP8X4),
                     rhs_scale=v_scales[4 * a :, cols],
                     start=(a == 0),
@@ -178,75 +179,91 @@ def tile_list_committee_award_scores_kernel(
                     left1[i][:],
                     ALU.mult,
                 )
-            if t > 0:
+            if t > 1:
                 left3 = third_pick(t - 1, slice(0, S3))
             left2 = ring.tile([P, S2], F32, name="left2", tag="left2", bufs=2)
             right2 = ring.tile([P, S2], F32, name="right2", tag="right2", bufs=2)
             a2[t] = ring.tile([P, S2], F32, name="a2", tag="a2", bufs=2)
             nc.vector.tensor_copy(left2[:], a1[:].indirect(p3[:]))
             nc.vector.tensor_copy(right2[:], a1[:].indirect(p4[:]))
-            if t > 0:
+            if t > 1:
                 third_sum(t - 1, slice(0, S3), left3[:])
             nc.vector.tensor_tensor(a2[t][:], left2[:], right2[:], ALU.max)
+            if t == 0:
+                third_sum(t, slice(0, S3), third_pick(t, slice(0, S3))[:])
 
         levels(0)
 
-        units = [(t, s) for t in range(1, PACK) for s in range(SLICES)]
+        units = [(t, d) for t in range(1, PACK) for d in range(SLICES // 2)]
         state = {}
 
         def multiply(u):
-            t, s = units[u]
-            bank = psum.tile([P, BLOCKS, P], F32, name="product", tag=f"bank{4 + u % 2}")
-            for b in range(BLOCKS):
-                cols = slice(s * BANK + b * P, s * BANK + (b + 1) * P)
-                for a in range(PASSES):
-                    nc.tensor.matmul_mx(
-                        out=bank[:, b, :],
-                        lhsT=v_words[a][:, cols].bitcast(FP8X4),
-                        lhsT_scale=v_scales[4 * a :, cols],
-                        rhs=w1_codes[a, t][:].bitcast(FP8X4),
-                        rhs_scale=w1_scales[a, t][:],
-                        start=(a == 0),
-                        stop=(a == PASSES - 1),
-                    )
-            turns = ring.tile([P, BANK], F32, name="turns", tag="turns")
-            nc.scalar.activation(turns[:], bank[:].rearrange("p b m -> p (b m)"), ACT.Abs, scale=TURN)
+            t, d = units[u]
+            turns = wide.tile([P, 2 * BANK], F32, name="wide_turns")
+            for e in range(2):
+                bank = psum.tile([P, BLOCKS, P], F32, name="product", tag=f"bank{4 * ((u + 1) % 2) + e}")
+                for b in range(BLOCKS):
+                    first = (2 * d + e) * BANK + b * P
+                    cols = slice(first, first + P)
+                    for a in range(PASSES):
+                        nc.tensor.matmul_mx(
+                            out=bank[:, b, :],
+                            lhsT=v_words[a][:, cols].bitcast(FP8X4),
+                            lhsT_scale=v_scales[4 * a :, cols],
+                            rhs=w1_codes[a, t].bitcast(FP8X4),
+                            rhs_scale=w1_scales[a, t],
+                            start=(a == 0),
+                            stop=(a == PASSES - 1),
+                        )
+                nc.scalar.activation(
+                    turns[:, e * BANK : (e + 1) * BANK], bank[:].rearrange("p b m -> p (b m)"), ACT.Abs, scale=TURN
+                )
             state[u] = turns
 
         def count(u):
             turns = state[u]
-            whole = ring.tile([P, BANK], U32, name="whole", tag="whole")
+            whole = wide.tile([P, 2 * BANK], U32, name="wide_whole")
             nc.scalar.activation(whole[:], turns[:], ACT.Copy, bias=-0.25)
             state[u] = (turns, whole)
 
         def subtract(u):
             turns, whole = state[u]
-            minus = ring.tile([P, BANK], F32, name="minus", tag="rest")
+            minus = wide.tile([P, 2 * BANK], F32, name="wide_minus")
             nc.scalar.activation(minus[:], whole[:], ACT.Copy, scale=-1.0, bias=-0.25)
-            bank = psum.tile([P, BLOCKS, P], F32, name="turned", tag=f"bank{6 + u % 2}")
-            for b in range(BLOCKS):
-                cols = slice(b * P, (b + 1) * P)
-                nc.tensor.matmul(bank[:, b, :], turns[:, cols], ident[:], start=True, stop=False, is_transpose=True)
-                nc.tensor.matmul(bank[:, b, :], minus[:, cols], ident[:], start=False, stop=True, is_transpose=True)
-            state[u] = bank
+            banks = []
+            for e in range(2):
+                bank = psum.tile([P, BLOCKS, P], F32, name="turned", tag=f"bank{4 * ((u + 1) % 2) + 2 + e}")
+                for b in range(BLOCKS):
+                    cols = slice(e * BANK + b * P, e * BANK + (b + 1) * P)
+                    nc.tensor.matmul(bank[:, b, :], turns[:, cols], ident[:], start=True, stop=False, is_transpose=True)
+                    nc.tensor.matmul(bank[:, b, :], minus[:, cols], ident[:], start=False, stop=True, is_transpose=True)
+                banks.append(bank)
+            state[u] = banks
 
         def cosine(u):
-            t, s = units[u]
-            nc.scalar.activation(
-                h[t][:, s * BANK : (s + 1) * BANK],
-                state[u][:].rearrange("p b m -> p (b m)"),
-                ACT.Sin,
-                scale=-2.0 * math.pi,
-            )
-            if s == SLICES - 1:
+            t, d = units[u]
+            for e in range(2):
+                first = (2 * d + e) * BANK
+                nc.scalar.activation(
+                    h[t][:, first : first + BANK],
+                    state[u][e][:].rearrange("p b m -> p (b m)"),
+                    ACT.Sin,
+                    scale=-2.0 * math.pi,
+                )
+            if d == SLICES // 2 - 1:
                 levels(t)
 
-        stages = [multiply, count, subtract, cosine]
-        for step in range(len(units) + len(stages) - 1):
-            for lag in reversed(range(len(stages))):
-                u = step - lag
-                if 0 <= u < len(units):
-                    stages[lag](u)
+        multiply(0)
+        for u in range(0, len(units), 2):
+            count(u)
+            multiply(u + 1)
+            subtract(u)
+            count(u + 1)
+            subtract(u + 1)
+            cosine(u)
+            if u + 2 < len(units):
+                multiply(u + 2)
+            cosine(u + 1)
 
         last = PACK - 1
         halves = [slice(i * P, (i + 1) * P) for i in range(S3 // P)]
@@ -271,11 +288,12 @@ def tile_list_committee_award_scores_kernel(
         for cols in halves:
             gained_tanh(last, cols)
         out_rows = out.rearrange("(p t) j -> p t j", t=PACK)
+        banks = []
         z16 = [keep.tile([P, P, PACK], BF16, name=f"z16_{i}", align_bytes=64) for i in range(len(halves))]
         for i, cols in enumerate(halves):
-            nc.vector.tensor_copy(z16[i][:], z32[:, :, cols].rearrange("p t j -> p j t"))
-        banks = []
-        for i, cols in enumerate(halves):
+            nc.vector.tensor_copy(
+                z16[i][:].rearrange("p (c e) t -> p c t e", e=4), z32[:, :, cols].rearrange("p t (c e) -> p c t e", e=4)
+            )
             z_codes = keep.tile([P, P], U32, name=f"z_codes{i}", align_bytes=64)
             z_scales = keep.tile([P, P], U8, name=f"z_scales{i}", align_bytes=64)
             nc.vector.quantize_mx(

@@ -47,11 +47,6 @@ def tile_list_committee_award_scores_kernel(
 
         scale_window = keep.tile([P, T], U8, name="scale_window", align_bytes=64)
         nc.vector.memset(scale_window[:].bitcast(I32), 0)
-        for q in range(QUADRANTS):
-            nc.sync.dma_start(
-                scale_window[32 * q : 32 * q + 4 * PASSES, :].bitcast(I32),
-                tab_scales[:, 4 * q : 4 * q + 4, :].bitcast(I32),
-            )
         offs_t = load_list(offs, "offs_t")
         w4_raw = keep.tile([P, 2 * H], U8, name="w4_raw", align_bytes=64)
         nc.sync.dma_start(w4_raw[:].bitcast(I32), w4_words[0].bitcast(I32))
@@ -61,12 +56,19 @@ def tile_list_committee_award_scores_kernel(
             nc.sync.dma_start(win[:], tab_words[a].rearrange("p t i -> p (t i)").bitcast(I32))
             return win
 
-        word_window = [load_words(0)]
-        w1_raw = []
-        for a in range(PASSES):
+        def load_w1(a):
             raw = keep.tile([P, PACK, H], F32, name=f"w1_raw{a}", align_bytes=64)
             nc.sync.dma_start(raw[:], w1[512 * a : 512 * (a + 1), :].rearrange("(p i) c -> p i c", i=PACK))
-            w1_raw.append(raw)
+            return raw
+
+        word_window = [load_words(0)]
+        w1_raw = [load_w1(0)]
+        for q in range(QUADRANTS):
+            nc.sync.dma_start(
+                scale_window[32 * q : 32 * q + 4 * PASSES, :].bitcast(I32),
+                tab_scales[:, 4 * q : 4 * q + 4, :].bitcast(I32),
+            )
+        w1_raw.append(load_w1(1))
         word_window.append(load_words(1))
         p1, p2 = load_list(pos1, "p1"), load_list(pos2, "p2")
         w4_scale_raw = keep.tile([P, H], U8, name="w4_scale_raw", align_bytes=64)
@@ -255,8 +257,8 @@ def tile_list_committee_award_scores_kernel(
 
         multiply(0)
         for u in range(0, len(units), 2):
-            count(u)
             multiply(u + 1)
+            count(u)
             subtract(u)
             count(u + 1)
             subtract(u + 1)

import math
from contextlib import ExitStack

import concourse.mybir as mybir
from concourse.masks import make_identity

K, H, T, S, S1, S2, S3 = 1024, 512, 4096, 2048, 1024, 512, 256
FLOPS = 2 * K * H * S + 2 * H * H * S3

F32 = mybir.dt.float32
BF16 = mybir.dt.bfloat16
I32 = mybir.dt.int32
U32 = mybir.dt.uint32
U16 = mybir.dt.uint16
U8 = mybir.dt.uint8
FP8X4 = mybir.dt.float8_e4m3fn_x4
FP4X4 = mybir.dt.float4_e2m1fn_x4
ALU = mybir.AluOpType
ACT = mybir.ActivationFunctionType

P = 128
PACK = 4
PASSES = K // (P * PACK)
BANK = 512
SLICES = S // BANK
BLOCKS = BANK // P
QUADRANTS = 4
SCALAR_SLICES = 3
TURN = 1.0 / (2.0 * math.pi)


def tile_list_committee_award_scores_kernel(
    tc, tab_words, tab_scales, w1, w4_words, w4_scales, gain, offs, pos1, pos2, pos3, pos4, pos5, pos6, out
):
    nc = tc.nc
    with ExitStack() as ctx:
        lists = ctx.enter_context(tc.tile_pool(name="lists", bufs=1))
        keep = ctx.enter_context(tc.tile_pool(name="keep", bufs=1))
        ring = ctx.enter_context(tc.tile_pool(name="ring", bufs=4))
        wide = ctx.enter_context(tc.tile_pool(name="wide", bufs=3))
        psum = ctx.enter_context(tc.psum_pool(name="psum", bufs=1))

        def load_list(src, name):
            tile = lists.tile(list(src.shape), U16, name=name)
            nc.sync.dma_start(tile[:], src)
            return tile

        scale_window = keep.tile([P, T], U8, name="scale_window", align_bytes=64)
        nc.vector.memset(scale_window[:].bitcast(I32), 0)
        offs_t = load_list(offs, "offs_t")
        w4_raw = keep.tile([P, 2 * H], U8, name="w4_raw", align_bytes=64)
        nc.sync.dma_start(w4_raw[:].bitcast(I32), w4_words[0].bitcast(I32))

        def load_words(a):
            win = keep.tile([P, T], I32, name=f"word_window{a}", align_bytes=64)
            nc.sync.dma_start(win[:], tab_words[a].rearrange("p t i -> p (t i)").bitcast(I32))
            return win

        def load_w1(a):
            raw = keep.tile([P, PACK, H], F32, name=f"w1_raw{a}", align_bytes=64)
            nc.sync.dma_start(raw[:], w1[512 * a : 512 * (a + 1), :].rearrange("(p i) c -> p i c", i=PACK))
            return raw

        word_window = [load_words(0)]
        w1_raw = [load_w1(0)]
        for q in range(QUADRANTS):
            nc.sync.dma_start(
                scale_window[32 * q : 32 * q + 4 * PASSES, :].bitcast(I32),
                tab_scales[:, 4 * q : 4 * q + 4, :].bitcast(I32),
            )
        w1_raw.append(load_w1(1))
        word_window.append(load_words(1))
        p1, p2 = load_list(pos1, "p1"), load_list(pos2, "p2")
        w4_scale_raw = keep.tile([P, H], U8, name="w4_scale_raw", align_bytes=64)
        nc.vector.memset(w4_scale_raw[:].bitcast(I32), 0)
        for q in range(QUADRANTS):
            nc.sync.dma_start(
                w4_scale_raw[32 * q : 32 * q + 4, :].bitcast(I32), w4_scales[0, 4 * q : 4 * q + 4, :].bitcast(I32)
            )
        p3, p4 = load_list(pos3, "p3"), load_list(pos4, "p4")
        p5, p6 = load_list(pos5, "p5"), load_list(pos6, "p6")
        gain_t = keep.tile([P, PACK], F32, name="gain_t")
        nc.sync.dma_start(gain_t[:], gain.rearrange("(p t) -> p t", t=PACK))
        ident = keep.tile([P, P], F32, name="ident")
        make_identity(nc, ident[:])
        warm = keep.tile([P, 1], F32, name="warm")
        nc.scalar.activation(warm[:], ident[:, 0:1], ACT.Silu)

        v_scales = keep.tile([P, S], U8, name="v_scales", align_bytes=64)
        v_words = [keep.tile([P, S], U32, name=f"v_words{a}", align_bytes=64) for a in range(PASSES)]
        nc.vector.tensor_copy(v_words[0][:], word_window[0][:].bitcast(U32).indirect(offs_t[:]))
        cols_per_slice = BANK // 16
        nc.vector.tensor_copy(v_scales[:], scale_window[:].indirect(offs_t[:]))
        for s in range(SLICES):
            nc.vector.tensor_copy(
                v_words[1][:, s * BANK : (s + 1) * BANK],
                word_window[1][:].bitcast(U32).indirect(offs_t[:, s * cols_per_slice : (s + 1) * cols_per_slice]),
            )

        w1_codes, w1_scales = {}, {}

        for a in range(PASSES):
            grouped = keep.tile([P, PACK, P, PACK], BF16, name=f"grouped{a}", align_bytes=64)
            nc.scalar.copy(
                grouped[:].rearrange("p t m i -> p m t i"), w1_raw[a][:].rearrange("p i (m t) -> p m t i", t=PACK)
            )
            codes = keep.tile([P, H], U32, name=f"w1_codes{a}", align_bytes=64)
            scales = keep.tile([P, H], U8, name=f"w1_scales{a}", align_bytes=64)
            nc.vector.quantize_mx(
                out=codes[:].bitcast(FP8X4), scales=scales[:], in_=grouped[:].rearrange("p t m i -> p (t m i)")
            )
            for t in range(PACK):
                w1_codes[a, t], w1_scales[a, t] = codes[:, t * P : (t + 1) * P], scales[:, t * P : (t + 1) * P]

        h = [keep.tile([P, S], F32, name=f"h{t}", tag=f"h{t}", align_bytes=64) for t in range(PACK)]

        direct = [psum.tile([P, BANK], F32, name=f"direct{s}", tag=f"bank{s}") for s in range(SLICES)]
        for a in range(PASSES):
            for s in range(SLICES):
                cols = slice(s * BANK, (s + 1) * BANK)
                nc.tensor.matmul_mx(
                    out=direct[s][:],
                    lhsT=w1_codes[a, 0].bitcast(FP8X4),
                    lhsT_scale=w1_scales[a, 0],
                    rhs=v_words[a][:, cols].bitcast(FP8X4),
                    rhs_scale=v_scales[4 * a :, cols],
                    start=(a == 0),
                    stop=(a == PASSES - 1),
                )
        for s in range(SLICES):
            cols = slice(s * BANK, (s + 1) * BANK)
            whole = ring.tile([P, BANK], U32, name="whole", tag="whole")
            rest = ring.tile([P, BANK], F32, name="rest", tag="rest")
            if s < SCALAR_SLICES:
                turns = ring.tile([P, BANK], F32, name="turns", tag="turns")
                nc.scalar.activation(turns[:], direct[s][:], ACT.Abs, scale=TURN)
                nc.scalar.activation(whole[:], turns[:], ACT.Copy, bias=-0.25)
                nc.vector.scalar_tensor_tensor(
                    rest[:], turns[:], 0.25, whole[:].bitcast(I32), ALU.subtract, ALU.subtract
                )
                nc.scalar.activation(h[0][:, cols], rest[:], ACT.Sin, scale=-2.0 * math.pi)
            else:
                nc.vector.tensor_scalar(whole[:].bitcast(I32), direct[s][:], TURN, -0.25, ALU.mult, ALU.add)
                nc.vector.scalar_tensor_tensor(
                    rest[:], direct[s][:], TURN, whole[:].bitcast(I32), ALU.mult, ALU.subtract
                )
                nc.scalar.activation(h[0][:, cols], rest[:], ACT.Sin, scale=-2.0 * math.pi, bias=0.5 * math.pi)

        w4_codes = keep.tile([P, 2 * H], U8, name="w4_codes", align_bytes=64)
        nc.vector.tensor_copy(
            w4_codes[:].rearrange("p (t m b) -> p t m b", t=PACK, b=2),
            w4_raw[:].rearrange("p (m t b) -> p t m b", t=PACK, b=2),
        )

        a3 = keep.tile([P, PACK, S3], F32, name="a3", align_bytes=64)

        a2 = {}
        half1 = S1 // 2

        def third_pick(t, cols):
            left3 = ring.tile([P, cols.stop - cols.start], F32, name="left3", tag="left0", bufs=1)
            nc.vector.tensor_copy(left3[:], a2[t][:].indirect(p5[:, cols.start // 16 : cols.stop // 16]))
            return left3

        def third_sum(t, cols, left3):
            nc.vector.tensor_tensor(
                a3[:, t, cols], a2[t][:].indirect(p6[:, cols.start // 16 : cols.stop // 16]), left3, ALU.add
            )

        def levels(t):
            a1 = ring.tile([P, S1], F32, name="a1", tag="a1", bufs=2)
            left1 = []
            for i in range(2):
                left = ring.tile([P, half1], F32, name="left1", tag=f"left{i}", bufs=1)
                nc.vector.tensor_copy(left[:], h[t][:].indirect(p1[:, i * half1 // 16 : (i + 1) * half1 // 16]))
                left1.append(left)
            for i in range(2):
                nc.vector.tensor_tensor(
                    a1[:, i * half1 : (i + 1) * half1],
                    h[t][:].indirect(p2[:, i * half1 // 16 : (i + 1) * half1 // 16]),
                    left1[i][:],
                    ALU.mult,
                )
            if t > 1:
                left3 = third_pick(t - 1, slice(0, S3))
            left2 = ring.tile([P, S2], F32, name="left2", tag="left2", bufs=2)
            right2 = ring.tile([P, S2], F32, name="right2", tag="right2", bufs=2)
            a2[t] = ring.tile([P, S2], F32, name="a2", tag="a2", bufs=2)
            nc.vector.tensor_copy(left2[:], a1[:].indirect(p3[:]))
            nc.vector.tensor_copy(right2[:], a1[:].indirect(p4[:]))
            if t > 1:
                third_sum(t - 1, slice(0, S3), left3[:])
            nc.vector.tensor_tensor(a2[t][:], left2[:], right2[:], ALU.max)
            if t == 0:
                third_sum(t, slice(0, S3), third_pick(t, slice(0, S3))[:])

        levels(0)

        units = [(t, d) for t in range(1, PACK) for d in range(SLICES // 2)]
        state = {}

        def multiply(u):
            t, d = units[u]
            turns = wide.tile([P, 2 * BANK], F32, name="wide_turns")
            for e in range(2):
                bank = psum.tile([P, BLOCKS, P], F32, name="product", tag=f"bank{4 * ((u + 1) % 2) + e}")
                for b in range(BLOCKS):
                    first = (2 * d + e) * BANK + b * P
                    cols = slice(first, first + P)
                    for a in range(PASSES):
                        nc.tensor.matmul_mx(
                            out=bank[:, b, :],
                            lhsT=v_words[a][:, cols].bitcast(FP8X4),
                            lhsT_scale=v_scales[4 * a :, cols],
                            rhs=w1_codes[a, t].bitcast(FP8X4),
                            rhs_scale=w1_scales[a, t],
                            start=(a == 0),
                            stop=(a == PASSES - 1),
                        )
                nc.scalar.activation(
                    turns[:, e * BANK : (e + 1) * BANK], bank[:].rearrange("p b m -> p (b m)"), ACT.Abs, scale=TURN
                )
            state[u] = turns

        def count(u):
            turns = state[u]
            whole = wide.tile([P, 2 * BANK], U32, name="wide_whole")
            nc.scalar.activation(whole[:], turns[:], ACT.Copy, bias=-0.25)
            state[u] = (turns, whole)

        def subtract(u):
            turns, whole = state[u]
            minus = wide.tile([P, 2 * BANK], F32, name="wide_minus")
            nc.scalar.activation(minus[:], whole[:], ACT.Copy, scale=-1.0, bias=-0.25)
            banks = []
            for e in range(2):
                bank = psum.tile([P, BLOCKS, P], F32, name="turned", tag=f"bank{4 * ((u + 1) % 2) + 2 + e}")
                for b in range(BLOCKS):
                    cols = slice(e * BANK + b * P, e * BANK + (b + 1) * P)
                    nc.tensor.matmul(bank[:, b, :], turns[:, cols], ident[:], start=True, stop=False, is_transpose=True)
                    nc.tensor.matmul(bank[:, b, :], minus[:, cols], ident[:], start=False, stop=True, is_transpose=True)
                banks.append(bank)
            state[u] = banks

        def cosine(u):
            t, d = units[u]
            for e in range(2):
                first = (2 * d + e) * BANK
                nc.scalar.activation(
                    h[t][:, first : first + BANK],
                    state[u][e][:].rearrange("p b m -> p (b m)"),
                    ACT.Sin,
                    scale=-2.0 * math.pi,
                )
            if d == SLICES // 2 - 1:
                levels(t)

        multiply(0)
        for u in range(0, len(units), 2):
            multiply(u + 1)
            count(u)
            subtract(u)
            count(u + 1)
            subtract(u + 1)
            cosine(u)
            if u + 2 < len(units):
                multiply(u + 2)
            cosine(u + 1)

        last = PACK - 1
        halves = [slice(i * P, (i + 1) * P) for i in range(S3 // P)]
        left3 = keep.tile([P, S3], F32, name="left3_last", tag="late", align_bytes=64)
        for cols in halves:
            nc.vector.tensor_copy(left3[:, cols], a2[last][:].indirect(p5[:, cols.start // 16 : cols.stop // 16]))
        for cols in halves:
            third_sum(last, cols, left3[:, cols])
        w4_scale = keep.tile([P, H], U8, name="w4_scale", tag="late", align_bytes=64)
        nc.vector.tensor_copy(
            w4_scale[:].rearrange("p (t m) -> p t m", t=PACK), w4_scale_raw[:].rearrange("p (m t) -> p t m", t=PACK)
        )
        z32 = keep.tile([P, PACK, S3], F32, name="z32", align_bytes=64)
        squashed = keep.tile([P, PACK, S3], F32, name="squashed", tag=f"h{last}", align_bytes=64)

        def gained_tanh(t, cols):
            nc.scalar.activation(squashed[:, t, cols], a3[:, t, cols], ACT.Tanh)
            nc.scalar.activation(z32[:, t, cols], squashed[:, t, cols], ACT.Copy, scale=gain_t[:, t : t + 1])

        for t in range(last):
            gained_tanh(t, slice(0, S3))
        for cols in halves:
            gained_tanh(last, cols)
        out_rows = out.rearrange("(p t) j -> p t j", t=PACK)
        banks = []
        z16 = [keep.tile([P, P, PACK], BF16, name=f"z16_{i}", align_bytes=64) for i in range(len(halves))]
        for i, cols in enumerate(halves):
            nc.vector.tensor_copy(
                z16[i][:].rearrange("p (c e) t -> p c t e", e=4), z32[:, :, cols].rearrange("p t (c e) -> p c t e", e=4)
            )
            z_codes = keep.tile([P, P], U32, name=f"z_codes{i}", align_bytes=64)
            z_scales = keep.tile([P, P], U8, name=f"z_scales{i}", align_bytes=64)
            nc.vector.quantize_mx(
                out=z_codes[:].bitcast(FP8X4), scales=z_scales[:], in_=z16[i][:].rearrange("p j t -> p (j t)")
            )
            for pair in range(PACK // 2):
                bank = psum.tile([P, 2, P], F32, name="y", tag=f"bank{2 * i + pair}")
                for e in range(2):
                    t = 2 * pair + e
                    nc.tensor.matmul_mx(
                        out=bank[:, e, :],
                        lhsT=w4_codes[:, 2 * P * t : 2 * P * (t + 1)].bitcast(FP4X4),
                        lhsT_scale=w4_scale[:, P * t : P * (t + 1)],
                        rhs=z_codes[:].bitcast(FP8X4),
                        rhs_scale=z_scales[:],
                        start=True,
                        stop=True,
                    )
                banks.append((bank, slice(2 * pair, 2 * pair + 2), cols))
        for n, (bank, rows, cols) in enumerate(banks):
            result = keep.tile([P, 2, P], F32, name=f"result{n}", align_bytes=64)
            nc.vector.tensor_tensor(result[:], bank[:], a3[:, rows, cols], ALU.add)
            queue = nc.sync if n % 2 == 0 else nc.scalar
            queue.dma_start(out_rows[:, rows, cols], result[:])
